import numpy as np, ml_dtypes
CORES = [40,64,80,88,96,104,120,144]
N = 8
import mx_ref
BF = ml_dtypes.bfloat16
def gentries(a):
    return np.ascontiguousarray(a.reshape(8, 16, -1).transpose(0, 2, 1)).reshape(8, -1)
def gtable(e):
    e = np.asarray(e); return np.ascontiguousarray(e.reshape(8, -1, 16).transpose(0, 2, 1)).reshape(128, -1).astype(np.int32)
def gcols(t, e):
    v = np.concatenate([t.reshape(8, 16, -1, 4), np.zeros((8, 16, 1, 4), BF)], axis=2)
    return np.ascontiguousarray(np.stack([v[g][:, e[g]] for g in range(8)])).reshape(128, -1)
def tile(rs):
    return np.stack(rs, axis=2).reshape(128, -1).astype(BF)
def pick(q, e):
    c = np.concatenate([q[0].reshape(128, -1, 4), np.zeros((128, 1, 4), np.uint8)], axis=1); s = np.concatenate([q[1], np.ones((16, 1), np.uint8)], axis=1)
    return (np.ascontiguousarray(c[:, e].reshape(128, -1)), np.ascontiguousarray(s[:, e]))
def join(*qs):
    return (np.concatenate([q[0] for q in qs], axis=1), np.concatenate([q[1] for q in qs], axis=1))
def put(q, e, v):
    c, s = q[0].reshape(128, -1, 4).copy(), q[1].copy(); c[:, e] = v[0].reshape(128, -1, 4); s[:, e] = v[1]
    return (c.reshape(128, -1), s)
def pk(c, s):
    return (np.ascontiguousarray(c), mx_ref.live(s))
def emit(q):
    return q[0], q[1]
def packed(v, rng):
    q = [mx_ref.quantize(np.ascontiguousarray(v[r])) for r in range(N)]
    return np.stack([a for a, b in q]), np.stack([mx_ref.plane(b, rng) for a, b in q])
def values_of_codes():
    e, c = np.zeros((128, 128, 4), np.float32), np.zeros((128, 2, 4), np.uint8)
    e[np.arange(128), np.arange(128), 0] = 1
    c[:127, :, 0] = np.arange(256).reshape(2, 128).T[:127]
    return mx_ref.matmul(mx_ref.quantize(e.reshape(128, 512).astype(BF)), (c.reshape(128, 8), np.full((16, 2), 127, np.uint8))).T.reshape(-1).astype(np.float64)
CODE_VALUE, SCALE_VALUE = values_of_codes(), 2.0 ** (np.arange(256) - 127.0)
def decode(q):
    return (CODE_VALUE[q[0]].reshape(16, 8, -1, 4) * SCALE_VALUE[q[1]][:, None, :, None] + 0.0).reshape(128, -1).astype(np.float32)
def f(rng, *shape):
    return mx_ref.flush((rng.standard_normal(shape, dtype=np.float32) * np.exp2(rng.integers(-2, 3, shape[:-1] + (1,)))).astype(BF))
def wide(rng, *shape, cols=0):
    v = rng.standard_normal(shape, dtype=np.float32) * np.exp2(rng.integers(-12, 13, shape)).astype(np.float32)
    if cols: v *= np.repeat(np.exp2(rng.integers(-cols, cols + 1, shape[:-2] + (1, shape[-1] // 4))) * (rng.random(shape[:-2] + (1, shape[-1] // 4)) > 0.0625), 4, axis=-1).astype(np.float32)
    return mx_ref.flush(v.astype(BF))
C, G, E, K, S = 320, 10, 10, 32, 256
STRIDE = [4, 2, 1]
DIR = [(-1, 0), (-1, 1), (0, 1), (1, 1), (1, 0), (1, -1), (0, -1), (-1, -1)]
def around(e, h):
    return np.stack([np.roll(e[:, g].reshape(N * G, 32), (-h * DIR[g][0], -h * DIR[g][1]), axis=(0, 1)).reshape(N, C) for g in range(8)], axis=1)
def numbers_of(rng):
    return {"x": np.array(f(rng, N, 128, 4 * C)), "u": np.array(f(rng, N, 128, 512)), "v": np.array(f(rng, N, 128, 512))}
def pointers(rng):
    return np.stack([gtable(rng.integers(0, S, (8, C))) for r in range(N)])
def same(rng, w):
    c, s = packed(np.stack([w] * N), rng)
    return {"wc": c, "ws": np.stack([s[0]] * N)}
def weights(rng, still=[]):
    w = np.array(f(rng, 128, 2048)).reshape(8, 16, 4, 8, 16, 4)
    for i in still:
        w[:, i] = 0
        w[:, :, :, :, i] = 0
    return same(rng, w.reshape(128, 2048))
def setup_inputs(rng):
    return {**numbers_of(rng), "p": pointers(rng), **weights(rng)}
def setup_inputs_ties(rng):
    d = numbers_of(rng)
    x = d["x"].reshape(N, 8, 16, C, 4)
    k = np.where(rng.random((N, 1, C)) < 0.5, 4, rng.integers(0, 3, (N, 1, C))) * np.ones((1, 8, 1))
    k[:, :, ::E] = rng.integers(0, 3, (N, 8, K))
    x[:, :, 0] = 0
    x[:, :, 0, :, 0] = k.astype(np.float32).astype(BF)
    u = d["u"].reshape(N, 128, 128, 4)
    u[:, :, ::16] = 0
    o = rng.permutation(N)
    for r in range(N):
        for h in range(0, 128, 16): u[r, h, h, 0] = 0.0 if r == o[0] else -1.0 if r == o[1] else 1.0
    return {"x": x.reshape(N, 128, 4 * C), "u": u.reshape(N, 128, 512), "v": d["v"], "p": pointers(rng), **weights(rng, [0])}
def setup_inputs_near(rng):
    d = numbers_of(rng)
    x = d["x"].astype(np.float32).reshape(N, 8, 16, C, 4)
    x[:, :, 0] = 0
    x[:, :, 8:] = 0
    x[:, :, 0, :, 0] = rng.integers(0, 2, (N, 1, C)) * 2.0 - 1.0
    x[:, :, 0, ::E] = 0
    s = rng.integers(0, 16, (N, 8, K))
    x[:, :, 8, ::E] = ((s[:, :, :, None] >> np.arange(4)) & 1) * np.exp2(np.arange(4) - 23.0)
    x[:, :, 10, :, 0] = (np.where(np.arange(8) < 4, -1.0, -1.125) * 2.0 ** -30)[:, None]
    x[:, :, 10, ::E, 0] = rng.integers(0, 2, (N, 8, K)) * 2.0 ** -30
    u = d["u"].reshape(N, 128, 128, 4)
    u[:, :, ::16] = 0
    o = rng.permutation(N) % 4
    for r in range(N):
        k = 1.0 if o[r] == 0 else 2.0 ** -30
        far = rng.permutation(8)
        if o[r] < 2:
            x[r, :, 11, :, 0] = -2.0 ** -10
            x[r, :, 11, ::E, 0] = 0
        for h in range(0, 128, 16):
            if o[r] < 2:
                u[r, h, h, 0] = k
                u[r, h + 11, h, 0] = k
            if o[r] == 2 and 16 * far[0] == h: u[r, h, h, 0] = 1.0
            if o[r] == 2 and 16 * far[1] == h: u[r, h, h, 0] = -1.0
            if o[r] < 3: u[r, h + 8, h] = k
            else: u[r, h + 10, h, 0] = k * 1.125 if h >= 64 else k * 1.25
    return {"x": x.reshape(N, 128, 4 * C).astype(BF), "u": u.reshape(N, 128, 512), "v": d["v"], "p": pointers(rng), **weights(rng, [0, 8, 9, 10, 11, 12, 13, 14, 15])}
def setup_inputs_huge(rng):
    d = numbers_of(rng)
    o = rng.permutation(N)
    c = rng.integers(0, 2, (N, 1, 1, C, 1)) * 2.0 - 1.0
    x = (0.6 + 0.09 * rng.random((N, 8, 16, C, 4))) * 2.0 ** 30 * c
    x[o == 0] = 0.875 * 2.0 ** 30 * c[o == 0]
    x[:, :, :, ::E] = (rng.random((N, 8, 1, K, 1)) * 2.0 - 1.0) * (0.8 + 0.2 * rng.random((N, 8, 16, K, 4))) * 2.0 ** 26
    a = 2.0 ** 29 * (1.0 - 0.1 * rng.random((N, 8, 16, 8, 4)))
    for g in range(8): a[:, g, :, g] *= 2.0
    for r in range(N):
        if o[r] == 0:
            a[r] = 2.0 ** 30
            for g in range(8): a[r, 0, :7 - g, g] *= 0.5
        if o[r] < N // 2: a[r] *= (rng.permutation(8) % 2 * 2.0 - 1.0)[None, None, :, None]
    u = d["u"].reshape(N, 128, 128, 4)
    u[:, :, ::16] = a.reshape(N, 128, 8, 4).astype(np.float32).astype(BF)
    w = np.zeros((128, 4, 128, 4), np.float32)
    i = np.arange(128)
    for b in range(4): w[i, b, i, b] = 4
    return {"x": x.astype(np.float32).reshape(N, 128, 4 * C).astype(BF), "u": u.reshape(N, 128, 512), "v": d["v"], "p": pointers(rng), **same(rng, w.reshape(128, 2048).astype(BF))}
def setup_inputs_few(rng):
    d = numbers_of(rng)
    e = rng.permutation(N)
    t = K * e[0] + rng.integers(0, K, (N, 8, C))
    t[e[0]] = S - 1
    t[e[1]] = 0
    t[e[2]] = K * e[2] + rng.integers(0, K, (8, C))
    t[e[3]] = rng.integers(0, S, (8, 1))
    return {**d, "p": np.stack([gtable(t[r]) for r in range(N)]), **weights(rng)}
def setup_inputs_spread(rng):
    d = setup_inputs(rng)
    d["x"] = wide(rng, N, 128, 4 * C, cols=6)
    return d
def check_inputs(d):
    b = []
    for k in ("x", "u", "v"):
        a = np.abs(d[k].astype(np.float32))
        if not (np.isfinite(a).all() and ((a == 0) | (a >= 2.0 ** -30) & (a <= 2.0 ** 30)).all()): b.append("a value of " + k)
    if not ((d["p"] >= 0) & (d["p"] < S)).all(): b.append("an entry of p")
    if ((d["wc"] & 0x7F) == 0x7F).any(): b.append("a code of wc that is no number")
    for k in ("wc", "ws"):
        if (d[k] != d[k][:1]).any(): b.append(k + " isn't the same on all ranks")
    z = np.zeros((128, 4, 4), np.float32)
    z[:, 1] = 2.0 ** -30
    z[:, 2] = 2.0 ** 30
    c, s = emit(mx_ref.quantize(z.reshape(128, 16).astype(BF)))
    for r in range(N):
        a = mx_ref.live(d["ws"][r])
        if not ((a == s[0, 0]) | (a >= s[0, 1]) & (a <= s[0, 2])).all(): b.append("a scale of ws")
    return b
def reference(x, u, v, p, wc, ws):
    qu = [mx_ref.quantize(u[r]) for r in range(N)]
    lay = [pk(wc[r], ws[r]) for r in range(N)]
    now = [x[r] for r in range(N)]
    ptr = np.stack([gentries(p[r]) for r in range(N)])
    for h in STRIDE:
        own = [decode(mx_ref.quantize(now[r])) for r in range(N)]
        seeds = np.concatenate([own[r].reshape(128, C, 4)[:, ::E] for r in range(N)], axis=1).reshape(128, 4 * S).astype(BF)
        came, new = around(ptr, h), []
        for r in range(N):
            z = (gcols(seeds, came[r]).astype(np.float32) - own[r]).astype(BF)
            s = mx_ref.matmul(qu[r], mx_ref.quantize(z))[::16] + np.float32(0.0)
            new.append(np.take_along_axis(came[r], np.argsort(-s, axis=0, kind="stable"), axis=0))
        ptr = np.stack(new)
        again = around(ptr, h)
        for r in range(N):
            q = mx_ref.quantize(gcols(seeds, again[r]))
            now[r] = tile([np.maximum(mx_ref.matmul(pick(lay[r], np.arange(128 * b, 128 * b + 128)), q), np.float32(0.0)) * np.float32(0.015625) + own[r][:, b::4] for b in range(4)])
    y, op = np.zeros((N, 128, C), np.float32), np.zeros((N, 8, C), np.float32)
    oc, osc = np.zeros((N, 128, 4 * C), np.uint8), np.zeros((N, 16, C), np.uint8)
    for r in range(N):
        q = mx_ref.quantize(now[r])
        y[r] = mx_ref.matmul(mx_ref.quantize(v[r]), q)
        op[r] = ptr[r]
        oc[r], osc[r] = emit(q)
    return {"y": y, "op": op, "oc": oc, "osc": osc}

from concourse.bass import DstId, RemoteDMATransfer
from concourse.mybir import dt, AluOpType, ActivationFunctionType

A_ = AluOpType
F_ = ActivationFunctionType
N, C, S = 8, 320, 256
STRIDE = [4, 2, 1]
TURN = 64
CODES, PLANE = "float8_e4m3fn_x4", "uint8"
BF, F32, I32, U16 = "bfloat16", "float32", "int32", "uint16"

SBUF = {
    "xt": (4 * C, BF), "ut": (512, BF), "vt": (512, BF),
    "pt": (20, I32), "pa": (20, I32), "pb": (20, I32), "pc": (20, I32), "pv": (24, F32), "a0": (64, BF), "a1": (64, BF),
    "wq": (512, CODES), "wp": (512, PLANE), "qo": (C, CODES), "so": (C, PLANE),
    "qd": (32, CODES), "sd": (32, PLANE), "rq": (32, CODES), "rs": (32, PLANE),
    "uq": (128, CODES), "us": (128, PLANE), "upq": (128, CODES), "ups": (128, PLANE), "vq": (128, CODES), "vs": (128, PLANE),
    "et": (2048, BF), "idf": (128, F32), "ida": (128, F32), "idb": (128, BF), "eq": (512, CODES), "es": (512, PLANE),
    "bp": (4 * S, BF), "gt": (4 * C, BF), "zt": (4 * 384, BF), "qz": (384, CODES), "sz": (384, PLANE),
    "yt": (4 * 576, BF), "qy": (576, CODES), "sy": (576, PLANE), "xn": (4 * 576, BF), "tm": (4 * 576, F32),
    "cr": (192, F32), "fl": (192, BF), "s1": (192, BF), "nq": (256, BF), "s2": (256, BF), "nt": (32, BF),
    "d0": (192, BF), "d1": (192, BF), "d2": (192, BF), "tg": (256, BF), "i2": (384, F32), "o2": (384, F32),
    "si": (256, BF), "sw": (256, BF), "sg": (80, BF), "sc": (80, F32), "mk": (80, BF), "mkf": (80, F32), "rz": (80, BF),
    "na": (32, F32), "lt": (40, F32), "dk": (32, BF), "dr": (256, BF), "offl": (32, U16), "offp": (48, U16),
    "ci": (16, I32), "cf": (40, F32), "st": (144, F32), "ul": (144, U16),
    "k0": (32, F32), "k1": (32, F32), "k2": (32, F32), "k3": (32, F32), "k4": (32, F32), "k5": (32, F32), "k6": (32, F32),
    "k7": (32, F32), "k8": (32, F32), "j0": (32, I32), "j1": (32, I32), "j2": (32, I32),
    "o0": (32, I32), "o1": (32, I32), "o3": (32, I32), "o4": (32, I32), "opf": (32, F32), "yo": (C, F32),
}
SCRATCH = {_n: ("sbuf", [128, SBUF[_n][0]], SBUF[_n][1]) for _n in SBUF}
SCRATCH["ps"] = ("psum", [128, 4096], F32)
for _k in range(4):
    SCRATCH["qx%d" % _k] = ("sbuf", [128, 576], CODES)
    SCRATCH["sx%d" % _k] = ("sbuf", [128, 576], PLANE)
    SCRATCH["rl%d" % _k] = ("sbuf", [128, 256], BF)
    SCRATCH["rr%d" % _k] = ("sbuf", [128, 32], BF)

SEMAPHORES = ["eV", "eA", "eP", "eG", "ldx", "ldp", "ldu", "ldw", "ldv", "lt0", "lt1", "lt2", "outs",
              "ar0", "ar1", "ar2", "ar3", "arq", "ars", "snta", "sntb"]

L_SEED, L_A0, L_R0, L_OWN, L_NB, L_FIN, L_UP, L_NEQ, L_REP, L_SI, L_SF, L_END = 0, 2, 6, 8, 26, 44, 56, 64, 80, 96, 128, 140
ORDER = ["ar0", "arq", "ars", "ar1", "ar2", "ar3"]


def ones(m):
    return bin(m).count("1")


def routes(T, topo):
    out = []
    for r, c in enumerate(T.cores):
        near = [(r - 1) % N, (r + 1) % N]
        others = near + [q for q in range(N) if q != r and q not in near]
        far = [q for q in others if not topo.may_write(c, T.cores[q])]
        able = [k for k in topo.cores_of(c) if k not in T.cores and all(topo.may_write(k, T.cores[q]) for q in far)]
        able = sorted(able, key=lambda k: topo.die(k) != topo.die(c))[:2]
        out.append({"direct": [q for q in others if q not in far], "via": {q: able[i % len(able)] for i, q in enumerate(far)}})
    return out


def receivers(r, k):
    return [(r - 1) % N, (r + 1) % N] if k in ("ar0", "ar3") else [q for q in range(N) if q != r]


def message(T, topo, rt, r, k):
    c, to = T.cores[r], receivers(r, k)
    direct = [q for q in rt[r]["direct"] if q in to]
    helpers = {}
    for q in rt[r]["via"]:
        if q in to:
            helpers.setdefault(rt[r]["via"][q], []).append(q)
    off = topo.mask(c, T.cores[direct[0]]) if direct else 0
    on = (topo.mask(c, list(helpers)[0]) & ~off) if helpers else 0
    return direct, off, helpers, on


def landing(T, k, r, q):
    if k == "arq":
        return T["qx0"][:, 32 * r:32 * r + 32].bitcast(dt.uint8)
    if k == "ars":
        return T["sx0"][:, 32 * r:32 * r + 32]
    s = (r - q + 1) % N
    return T["rl" + k[2]][:, 32 * s:32 * s + 32]


def stopover(T, k):
    if k == "arq":
        return T["rq"][:, :].bitcast(dt.uint8)
    if k == "ars":
        return T["rs"][:, :]
    return T["rr" + k[2]][:, :]


def arrivals(T, topo, rt, k, q):
    return sum(ones(topo.mask(rt[r]["via"].get(q, T.cores[r]), T.cores[q])) for r in range(N) if r != q and q in receivers(r, k))


def dest(topo, d, s):
    rid, pid = topo.addr(d, s)
    return DstId(rid=rid, pnc=pid)


def helper_program(g, core, T, topo, rt):
    for r in range(N):
        if core not in rt[r]["via"].values():
            continue
        sent = 0
        for k in ORDER:
            direct, off, helpers, on = message(T, topo, rt, r, k)
            if core not in helpers:
                continue
            qs = helpers[core]
            m = topo.mask(core, T.cores[qs[0]])
            g.wait_ge(T.sem[k], ones(on))
            g.remote_dma_fused([RemoteDMATransfer(dst_ids=[dest(topo, T.cores[q], core) for q in qs], dma_engine_mask=m,
                                                  remote_sem=T.sem[k], srcs=[stopover(T, k)],
                                                  dsts=[landing(T, k, r, q) for q in qs])], local_sem=T.sem["sntb"])
            sent += ones(m)
        g.wait_ge(T.sem["sntb"], sent)


def rank_program(g, core, T, topo):
    rt = routes(T, topo)
    rank = T.rank_of(core)
    if rank is None:
        helper_program(g, core, T, topo, rt)
        return

    Q = {"V": g.vector, "A": g.scalar, "P": g.tensor, "G": g, "S": g.sync}
    count = {"V": 0, "A": 0, "P": 0, "G": 0}
    waited = {q: {} for q in Q}
    log = {}
    total = {}

    def vw(name, c0, c1, st=1, p0=0, p1=128):
        ap_ = T[name][p0:p1, c0:c1] if st == 1 else T[name][p0:p1, c0:c1:st]
        return (ap_, [(name, p0, p1, frozenset(range(c0, c1, st)))])

    def words(v):
        return (v[0].bitcast(dt.uint32), v[1])

    def octets(v):
        return (v[0].bitcast(dt.uint8), v[1])

    def ind(win, off):
        return (win[0].indirect(off[0]), win[1] + off[1])

    def wait(q, sem, val):
        if waited[q].get(sem, 0) < val:
            Q[q].wait_ge(T.sem[sem], val)
            waited[q][sem] = val

    def order(q, reads, writes, token):
        need = {}
        mine = [(r, False) for v in reads for r in v[1]] + [(r, True) for v in writes for r in v[1]]
        for (name, p0, p1, cols), wr in mine:
            for (a0, a1, ac, awr, aq, tok) in log.get(name, []):
                if name == "ps":
                    hit = min(cols) // 512 == min(ac) // 512 and (aq != q or wr or awr)
                else:
                    hit = (wr or awr) and a0 < p1 and p0 < a1 and not cols.isdisjoint(ac)
                if hit and tok != token:
                    need[tok[0]] = max(need.get(tok[0], 0), tok[1])
        for sem in need:
            wait(q, sem, need[sem])
        for (name, p0, p1, cols), wr in mine:
            log.setdefault(name, []).append((p0, p1, cols, wr, q, token))

    def run(q, reads, writes, call):
        count[q] += 1
        order(q, [r for r in reads if isinstance(r, tuple)], writes, ("e" + q, count[q]))
        call().then_inc(T.sem["e" + q], 1)

    def ap(x):
        return x[0] if isinstance(x, tuple) else x

    def dma(q, out, in_, sem, n):
        total[sem] = 16 * n
        order(q, [in_], [out], (sem, 16 * n))
        Q[q].dma_start(out[0], in_[0]).then_inc(T.sem[sem], 16)

    def hbm(a):
        return (a, [])

    def ts(out, in0, s1, s2, op0, op1=None):
        if op1 is None:
            run("V", [in0, s1], [out], lambda: g.vector.tensor_scalar(out[0], in0[0], ap(s1), None, op0))
        else:
            run("V", [in0, s1, s2], [out], lambda: g.vector.tensor_scalar(out[0], in0[0], ap(s1), ap(s2), op0, op1))

    def tt(out, a, b, op):
        run("V", [a, b], [out], lambda: g.vector.tensor_tensor(out[0], a[0], b[0], op))

    def cp(q, out, a):
        if q == "V":
            run("V", [a], [out], lambda: g.vector.tensor_copy(out[0], a[0]))
        else:
            run("A", [a], [out], lambda: g.scalar.activation(out[0], a[0], F_.Copy))

    def act(out, a, func, scale, bias=0.0):
        run("A", [a, scale, bias], [out], lambda: g.scalar.activation(out[0], a[0], func, bias=ap(bias), scale=ap(scale)))

    def fill(out, val):
        run("V", [], [out], lambda: g.vector.memset(out[0], val))

    def iota(out, pat, base, cm=0, small=True):
        if small:
            run("G", [], [out], lambda: g.iota(out[0], pat, base, cm, allow_small_or_imprecise_dtypes=True))
        else:
            run("G", [], [out], lambda: g.iota(out[0], pat, base, cm))

    def keep_unless(out, a, pat, base, val):
        run("G", [a], [out], lambda: g.affine_select(out[0], a[0], pat, A_.not_equal, val, base, 0))

    def turn(out, a):
        run("V", [a], [out], lambda: g.vector.transpose(out[0], a[0]))

    def scan(out, a, b):
        run("V", [a, b], [out], lambda: g.vector.tensor_tensor_scan(out[0], a[0], b[0], 0.0, A_.mult, A_.add))

    def quant(qn, sn, c0, tile, t0, n):
        a, b, c = vw(qn, c0, c0 + n), vw(sn, c0, c0 + n), vw(tile, 4 * t0, 4 * (t0 + n))
        run("V", [c], [a, b], lambda: g.vector.quantize_mx(a[0], b[0], c[0]))

    def mm(bk, lq, ls, l0, mq, ms, m0, n):
        o, a, b, c, d = vw("ps", 512 * bk, 512 * bk + n), vw(lq, l0, l0 + 128), vw(ls, l0, l0 + 128), vw(mq, m0, m0 + n), vw(ms, m0, m0 + n)
        run("P", [a, b, c, d], [o], lambda: g.tensor.matmul_mx(o[0], a[0], b[0], c[0], d[0], True, True))

    def bank(b, c0, c1):
        return vw("ps", 512 * b + c0, 512 * b + c1)

    def lst(c0, n):
        return vw("ul", c0, c0 + n)

    def col(name, c):
        return vw(name, c, c + 1)

    def send(k, src, lsem):
        direct, off, helpers, on = message(T, topo, rt, rank, k)
        order("G", [src], [], (lsem, 1 << 20))
        xs = []
        if helpers:
            xs.append(RemoteDMATransfer(dst_ids=[dest(topo, h, core) for h in helpers], dma_engine_mask=on, remote_sem=T.sem[k],
                                        srcs=[src[0]], dsts=[stopover(T, k) for h in helpers]))
        if direct:
            xs.append(RemoteDMATransfer(dst_ids=[dest(topo, T.cores[q], core) for q in direct], dma_engine_mask=off, remote_sem=T.sem[k],
                                        srcs=[src[0]], dsts=[landing(T, k, rank, q) for q in direct]))
        g.remote_dma_fused(xs, local_sem=T.sem[lsem])
        total[lsem] = total.get(lsem, 0) + ones(on) + ones(off)
        total[k] = arrivals(T, topo, rt, k, rank)
        name = {"arq": "qx0", "ars": "sx0"}.get(k, "rl" + k[2])
        own = rank if k in ("arq", "ars") else 1
        cols = frozenset(range(256)) - frozenset(range(32 * own, 32 * own + 32))
        log.setdefault(name, []).append((0, 128, cols, True, "R", (k, total[k])))

    dma("A", vw("pt", 0, 20), hbm(T["p"][:, :]), "ldp", 1)
    dma("S", vw("xt", 4 * TURN, 4 * C), hbm(T["x"][:, 0:4 * (C - TURN)]), "ldx", 2)
    dma("S", vw("xt", 0, 4 * TURN), hbm(T["x"][:, 4 * (C - TURN):4 * C]), "ldx", 2)
    wait("S", "ldx", 32)
    dma("S", vw("ut", 0, 512), hbm(T["u"][:, :]), "ldu", 1)

    iota(col("ci", 0), [[1, 1]], 0, 1, False)
    iota(col("ci", 1), [[1, 1]], 0, 13, False)
    iota(vw("k0", 0, 4), [[1, 2], [0, 2]], 0)
    iota(vw("idf", 0, 128), [[1, 128]], 0, -1)
    iota(vw("k5", 0, 8), [[0, 2], [2, 4]], 0)
    for c, v in ((0, 0), (1, 0), (2, 16), (3, 16), (4, 0), (5, 16)):
        iota(vw("k1", c, 24, 6), [[0, 4]], v)
    for i, h in enumerate(STRIDE):
        iota(vw("k2", 6 * i, 6 * i + 6), [[0, 6]], -h)
    iota(vw("k2", 18, 20), [[STRIDE[0] - STRIDE[1], 2]], -STRIDE[0])
    P_ = col("ci", 0)
    ts(col("ci", 2), col("ci", 1), 15, None, A_.bitwise_and)
    ts(col("ci", 3), P_, 15, None, A_.bitwise_and)
    ts(col("ci", 4), P_, 31, None, A_.bitwise_and)
    ts(col("ci", 5), P_, 4, None, A_.logical_shift_right)
    ts(col("st", L_SEED), col("ci", 2), 10.0, float(TURN), A_.mult, A_.add)
    ts(col("cf", 20), col("ci", 2), 10.0, -float(C), A_.is_ge, A_.mult)
    ts(col("cf", 21), col("ci", 3), 9.0, 2.0, A_.min, A_.mult)
    ts(col("cf", 22), col("ci", 3), 2.0, 20.0, A_.is_lt, A_.mult)
    ts(col("st", L_R0), col("ci", 4), 0.0, None, A_.add)
    ts(col("st", L_R0 + 1), col("ci", 4), 32.0, None, A_.add)
    ts(col("st", L_SEED + 1), col("cf", 20), col("st", L_SEED), 160.0, A_.add, A_.add)
    ts(col("cf", 23), col("cf", 22), col("cf", 21), -4.0, A_.add, A_.add)
    ts(col("ci", 6), P_, 5, None, A_.logical_shift_right)
    ts(vw("st", L_A0, L_A0 + 4), vw("k0", 0, 4), col("cf", 23), None, A_.add)
    ts(col("ci", 7), P_, 2, 1, A_.logical_shift_right, A_.bitwise_and)
    cp("V", vw("ul", 0, L_OWN), vw("st", 0, L_OWN))
    ts(col("ci", 8), P_, 7, None, A_.bitwise_and)
    ts(col("ci", 9), P_, 3, 1, A_.logical_shift_right, A_.bitwise_and)
    ts(col("ci", 10), P_, 16, None, A_.bitwise_and)
    ts(col("ci", 11), P_, 3, None, A_.bitwise_and)
    cp("V", vw("cf", 0, 12), vw("ci", 0, 12))
    R_, G_, R7, RH, E16 = col("cf", 3), col("cf", 5), col("cf", 8), col("cf", 9), col("cf", 10)
    ts(col("cf", 6), col("ci", 6), 2.0, col("cf", 7), A_.mult, A_.add)
    ts(col("cf", 16), G_, 1.0, None, A_.min)
    ts(col("cf", 17), G_, -3.0, 0.0, A_.add, A_.max)
    ts(vw("cf", 12, 14), vw("cf", 5, 7), -2.0, -1.0, A_.add, A_.max)
    ts(vw("cf", 14, 16), vw("cf", 5, 7), -5.0, 0.0, A_.add, A_.max)
    ts(col("cf", 18), col("cf", 17), 2.0, col("cf", 16), A_.min, A_.subtract)
    ts(vw("cf", 24, 26), vw("cf", 12, 14), 1.0, None, A_.min)
    act(vw("ida", 0, 128), vw("idf", 0, 128), F_.Abs, 1.0)
    act(vw("idb", 0, 128), vw("ida", 0, 128), F_.Relu, -1.0, 1.0)
    for b in range(4):
        for t in range(4):
            act(vw("et", 512 * b + t, 512 * b + 512, 4), vw("idb", 0, 128), F_.Copy, float(t == b))

    ts(vw("pa", 0, 20), vw("pt", 0, 20), 240, None, A_.bitwise_and)
    ts(vw("pb", 0, 20), vw("pt", 0, 20), 5.0, None, A_.mult)
    tt(vw("cf", 26, 28), vw("cf", 24, 26), vw("cf", 14, 16), A_.subtract)
    ts(vw("pc", 0, 20), vw("pb", 0, 20), 15, None, A_.bitwise_and)
    DR = col("cf", 26)
    ts(vw("k3", 0, 20), vw("k2", 0, 20), col("cf", 18), R_, A_.mult, A_.add)
    tt(vw("pv", 0, 20), vw("pa", 0, 20), vw("pc", 0, 20), A_.add)
    ts(vw("k1", 18, 20), vw("k1", 18, 20), R_, None, A_.add)
    cp("V", vw("a0", 0, 64), ind(vw("pv", 0, 20), lst(L_A0, 4)))
    turn(vw("a1", 0, 64), vw("a0", 0, 64))
    cp("V", vw("rl0", 32, 64), ind(vw("a1", 0, 64), lst(L_R0, 2)))
    send("ar0", vw("rl0", 32, 64), "snta")

    quant("qo", "so", 0, "xt", 0, C)
    cp("V", words(vw("qd", 0, 32)), ind(words(vw("qo", 0, C)), lst(L_SEED, 2)))
    cp("V", vw("sd", 0, 32), ind(vw("so", 0, C), lst(L_SEED, 2)))
    send("arq", octets(vw("qd", 0, 32)), "snta")
    send("ars", vw("sd", 0, 32), "snta")
    wait("S", "snta", total["snta"])
    dma("S", octets(vw("wq", 0, 512)), hbm(T["wc"][:, :]), "ldw", 2)
    dma("S", vw("wp", 0, 512), hbm(T["ws"][:, :]), "ldw", 2)
    iota(vw("o2", 0, 288), [[0, 288]], 0)
    iota(vw("lt", 0, 40), [[0, 40]], 0)
    iota(vw("zt", 4 * 256, 4 * 384), [[0, 512]], 0)
    iota(vw("d1", 0, 192), [[0, 192]], 1)
    keep_unless(vw("d2", 0, 192), vw("d1", 0, 192), [[0, 3], [1, 8], [1, 8]], -7, -1.0)
    keep_unless(vw("d0", 0, 192), vw("d2", 0, 192), [[0, 24], [1, 8]], 0, 0.0)
    iota(vw("tg", 0, 256), [[1, 8], [0, 4], [1, 8]], -6)

    tt(vw("k4", 0, 20), vw("k3", 0, 20), vw("k1", 0, 20), A_.add)
    ts(col("cf", 28), DR, 32.0, 32.0, A_.mult, A_.add)
    ts(vw("j0", 0, 20), vw("k4", 0, 20), 32.0, None, A_.add)
    ts(vw("j2", 0, 2), vw("k1", 4, 6), R_, 19.0, A_.add, A_.min)
    ts(vw("j1", 0, 20), vw("j0", 0, 20), 31, None, A_.bitwise_and)
    ts(col("cf", 19), col("ci", 11), 4.0, RH, A_.mult, A_.add)
    ts(vw("st", L_OWN, L_OWN + 18), vw("j1", 0, 18), 0.0, None, A_.add)
    ts(vw("st", L_NB, L_NB + 18), vw("j1", 0, 18), col("cf", 28), None, A_.add)
    ts(vw("j2", 4, 6), vw("j2", 0, 2), 1, None, A_.logical_shift_right)
    ts(vw("j2", 8, 10), vw("j2", 0, 2), 1, None, A_.bitwise_and)
    cp("V", vw("ul", L_OWN, L_FIN), vw("st", L_OWN, L_FIN))
    ts(vw("k6", 2, 4), vw("k5", 0, 2), col("cf", 19), 9.0, A_.add, A_.min)
    cp("V", vw("k6", 0, 2), vw("j2", 4, 6))
    ts(vw("k7", 0, 2), vw("j2", 8, 10), 32.0, E16, A_.mult, A_.add)
    ts(col("k7", 2), col("cf", 7), 16.0, 64.0, A_.mult, A_.add)
    ts(col("k7", 3), col("cf", 7), 16.0, 64.0, A_.mult, A_.add)
    ts(vw("k6", 4, 8), vw("k6", 0, 4), 2.0, 10.0, A_.is_lt, A_.mult)
    for i, h in enumerate(STRIDE):
        ts(vw("cf", 32 + 2 * i, 34 + 2 * i), vw("cf", 26, 28), float(h), 8.0, A_.mult, A_.add)
    tt(vw("k6", 8, 12), vw("k6", 4, 8), vw("k6", 0, 4), A_.add)
    cp("V", words(vw("qx0", 32 * rank, 32 * rank + 32)), ind(words(vw("qo", 0, C)), lst(L_SEED, 2)))
    cp("A", vw("sx0", 32 * rank, 32 * rank + 32), ind(vw("so", 0, C), lst(L_SEED, 2)))
    for i in range(3):
        ts(vw("k3", 4 * i, 4 * i + 2), vw("k6", 8, 10), col("cf", 32 + 2 * i), None, A_.add)
        ts(vw("k3", 4 * i + 2, 4 * i + 4), vw("k6", 10, 12), col("cf", 33 + 2 * i), None, A_.add)
    quant("eq", "es", 0, "et", 0, 512)
    ts(vw("k0", 0, 12), vw("k3", 0, 12), 8.0, -10.0, A_.is_ge, A_.mult)
    ts(vw("k2", 0, 12), vw("k3", 0, 12), 18.0, -10.0, A_.is_ge, A_.mult)
    ts(vw("k4", 0, 12), vw("k3", 0, 12), 10.0, -192.0, A_.is_ge, A_.mult)
    ts(vw("k8", 0, 12), vw("k3", 0, 12), 20.0, 192.0, A_.is_ge, A_.mult)
    for i in range(3):
        tt(vw("k3", 4 * i, 4 * i + 4), vw("k3", 4 * i, 4 * i + 4), vw("k7", 0, 4), A_.add)
    tt(vw("k0", 0, 12), vw("k0", 0, 12), vw("k2", 0, 12), A_.add)
    tt(vw("k4", 0, 12), vw("k4", 0, 12), vw("k8", 0, 12), A_.add)
    quant("qx0", "sx0", S, "xt", 0, C)
    tt(vw("k0", 0, 12), vw("k0", 0, 12), vw("k3", 0, 12), A_.add)
    ts(vw("k4", 0, 12), vw("k4", 0, 12), 194.0, None, A_.add)
    for b in range(4):
        mm(b, "eq", "es", 128 * b, "qx0", "sx0", S, C)
    tt(vw("st", L_FIN, L_FIN + 12), vw("k0", 0, 12), vw("k4", 0, 12), A_.add)
    ts(vw("k3", 0, 8), vw("k5", 0, 8), RH, None, A_.add)
    ts(col("cf", 12), R7, -8.0, None, A_.add)
    ts(col("cf", 13), R7, 1.0, None, A_.add)
    ts(vw("k2", 0, 8), vw("k3", 0, 8), R7, None, A_.add)
    act(col("cf", 14), R7, F_.Copy, 8.0, 7.0)
    act(col("cf", 15), R7, F_.Identity, 4.0, RH)
    act(col("cf", 16), RH, F_.Identity, 64.0, col("cf", 14))
    act(col("cf", 17), col("cf", 14), F_.Copy, 1.0, 128.0)
    act(col("cf", 31), col("cf", 15), F_.Copy, 1.0, 2.0)
    for c0, c in ((L_NEQ, 16), (L_NEQ + 1, 17), (L_REP, 15), (L_REP + 1, 31)):
        act(vw("st", c0, c0 + 15, 2), vw("k5", 0, 8), F_.Identity, 0.0, col("cf", c))
    ts(vw("k8", 0, 4), vw("k2", 0, 4), 8.0, col("cf", 12), A_.is_ge, A_.mult)
    ts(vw("k8", 4, 8), vw("k2", 4, 8), 6.0, col("cf", 13), A_.is_le, A_.mult)
    quant("uq", "us", 0, "ut", 0, 128)
    tt(vw("k8", 0, 8), vw("k8", 0, 8), vw("k3", 0, 8), A_.add)
    cp("V", vw("cf", 29, 31), vw("j1", 18, 20))
    ts(vw("st", L_UP, L_UP + 8), vw("k8", 0, 8), 16.0, None, A_.mult)
    cp("V", vw("ul", L_FIN, L_SI), vw("st", L_FIN, L_SI))

    def own_blocks(k):
        a, c0, n = {0: (96, 0, 6), 3: (0, 12, 4)}.get(k, (0, 6 * (k - 1), 12))
        cp("A", vw("i2", a, a + 16 * n), ind(vw("rl%d" % k, 32, 64), lst(L_OWN + c0, n)))
        turn(vw("o2", a, a + 16 * n), vw("i2", a, a + 16 * n))

    def next_gather(k):
        cp("A", vw("i2", 288, 384), ind(vw("rl%d" % k, 0, 96), lst(L_NB + 6 * k, 6)))

    def next_lists(k):
        turn(vw("o2", 288, 384), vw("i2", 288, 384))
        cp("V", vw("na", 0, 32), ind(vw("o2", 96, 384), lst(L_FIN + 4 * k + 2, 2)))
        cp("V", vw("offl", 0, 32), ind(vw("o2", 96, 384), lst(L_FIN + 4 * k, 2)))
        for q in range(4):
            for w in range(4):
                dma("S", vw("lt", 8 * w, 8 * w + 8, 1, 32 * q, 32 * q + 32), vw("na", 8 * q, 8 * q + 8, 1, 32 * w, 32 * w + 32), "lt%d" % k, 16)

    def again(rd):
        cp("V", vw("offp", 16, 48), ind(vw("o2", 0, 256), lst(L_FIN + 4 * rd, 2)))

    def pull(q, b, c0, n):
        cp(q, vw("yt", 4 * c0 + b, 4 * (c0 + n), 4), ind(vw("bp", S * b, S * b + S), vw("offp", c0 // 16, (c0 + n) // 16)))

    def layer(c0, n):
        quant("qy", "sy", c0, "yt", c0, n)
        for b in range(4):
            mm(4 + b, "wq", "wp", 128 * b, "qy", "sy", c0, n)

    def relu(b, c0, n):
        act(vw("tm", 576 * b + c0, 576 * b + c0 + n), bank(4 + b, 0, n), F_.Relu, 0.015625)

    def add(b, c0, n, f0):
        tt(vw("xn", 4 * c0 + b, 4 * (c0 + n), 4), vw("tm", 576 * b + c0, 576 * b + c0 + n), bank(b, f0, f0 + n), A_.add)

    def stores(s0, n):
        j = (s0 - TURN) % C
        todo = [(hbm(T["y"][:, j:j + n]), vw("yo", s0, s0 + n)),
                (hbm(T["oc"][:, 4 * j:4 * (j + n)]), octets(vw("qx3", S + s0, S + s0 + n)))]
        return todo + [(hbm(T["osc"][4 * k:4 * k + 4, j:j + n]), vw("sx3", S + s0, S + s0 + n, 1, 32 * k, 32 * k + 4)) for k in range(4)]

    NOUT = 16 + 18
    own_blocks(0)
    cp("V", words(vw("upq", 0, 128)), ind(words(vw("uq", 0, 128)), lst(L_UP, 8)))
    cp("A", vw("ups", 0, 128), ind(vw("us", 0, 128), lst(L_UP, 8)))
    next_gather(0)
    next_lists(0)
    quant("qz", "sz", 256, "zt", 256, 128)

    for rd in range(3):
        k = rd + 1
        qx, sx, qn, sn, rl = "qx%d" % rd, "sx%d" % rd, "qx%d" % k, "sx%d" % k, "rl%d" % k
        for b in range(4):
            mm(4 + b, "eq", "es", 128 * b, qx, sx, 0, S)
        if rd > 0:
            for b in range(4):
                mm(b, "eq", "es", 128 * b, qx, sx, S, C)

        def unpack(q, b):
            cp(q, vw("bp", S * b, S * b + S), bank(4 + b, 0, S))

        def gather(q, b):
            cp(q, vw("gt", C * b, C * b + C), ind(vw("bp", S * b, S * b + S), vw("offl", 0, 20)))

        def less(b):
            tt(vw("zt", b, 4 * C, 4), vw("gt", C * b, C * b + C), bank(b, 0, C), A_.subtract)

        unpack("V", 0)
        unpack("A", 1)
        unpack("V", 2)
        gather("A", 0)
        gather("V", 2)
        gather("A", 1)
        unpack("A", 3)
        less(0)
        less(2)
        gather("A", 3)
        less(1)
        tt(vw("dk", 0, 32), vw("lt", 0, 32), vw("lt", 4, 36), A_.subtract)
        cp("A", vw("dr", 0, 256), ind(vw("dk", 0, 32), lst(L_REP, 16)))
        less(3)
        quant("qz", "sz", 0, "zt", 0, 128)
        mm(4, "qz", "sz", 0, "upq", "ups", 0, 128)
        quant("qz", "sz", 128, "zt", 128, 192)
        mm(5, "qz", "sz", 128, "upq", "ups", 0, 128)
        mm(6, "qz", "sz", 256, "upq", "ups", 0, 128)
        for t in range(3):
            cp("A", vw("cr", 64 * t, 64 * t + 64), bank(4 + t, 64, 128))
            tt(vw("fl", 64 * t, 64 * t + 64), bank(4 + t, 0, 64), vw("cr", 64 * t, 64 * t + 64), A_.is_ge)
        scan(vw("s1", 0, 192), vw("d0", 0, 192), vw("fl", 0, 192))
        tt(vw("nq", 0, 256), ind(vw("s1", 0, 192), lst(L_NEQ, 16)), vw("tg", 0, 256), A_.not_equal)
        scan(vw("s2", 0, 256), vw("nq", 0, 256), vw("dr", 0, 256))
        for q in range(4):
            for w in range(4):
                cp("VA"[(q + w) % 2], vw("nt", q, 32, 4, 32 * w, 32 * w + 32), vw("s2", 64 * w + 7, 64 * w + 64, 8, 32 * q, 32 * q + 32))
        turn(vw(rl, 32, 64), vw("nt", 0, 32))
        send("ar%d" % k, vw(rl, 32, 64), "sntb")

        own_blocks(k)
        if rd == 0:
            dma("S", vw("vt", 0, 512), hbm(T["v"][:, :]), "ldv", 1)
            iota(vw("k5", 0, 16), [[32, 8], [0, 2]], 0)
            iota(vw("k4", 0, 12), [[0, 2], [16, 6]], 80 + (10 * (1 - rank)) % 80)
            iota(vw("mkf", 0, 80), [[0, 16], [1, 5]], 0)
            for i in range(2):
                ts(vw("st", L_SI + 16 * i, L_SI + 16 * i + 16), vw("k5", 0, 16), col("cf", 29 + i), None, A_.add)
                ts(col("cf", 12 + i), DR, float(STRIDE[i]), R_, A_.mult, A_.add)
            ts(col("j2", 0), col("ci", 2), 10.0, None, A_.mult)
            for i in range(2):
                ts(vw("k3", 6 * i, 6 * i + 6), vw("k4", 6 * i, 6 * i + 6), col("cf", 12 + i), None, A_.add)
            ts(col("j2", 1), col("j2", 0), 5, None, A_.logical_shift_right)
            ts(vw("k1", 0, 12), vw("k3", 0, 12), 80.0, -80.0, A_.is_ge, A_.mult)
            ts(vw("k2", 0, 12), vw("k3", 0, 12), 160.0, -80.0, A_.is_ge, A_.mult)
            cp("V", col("cf", 14), col("j2", 1))
            tt(vw("k1", 0, 12), vw("k1", 0, 12), vw("k2", 0, 12), A_.add)
            ts(vw("rz", 0, 80), vw("mkf", 0, 80), 0.0, None, A_.not_equal)
            tt(vw("k3", 0, 12), vw("k3", 0, 12), vw("k1", 0, 12), A_.add)
            ts(vw("mk", 0, 80), vw("mkf", 0, 80), col("cf", 14), None, A_.is_equal)
            ts(vw("k3", 0, 12), vw("k3", 0, 12), 79.0, None, A_.min)
            ts(vw("j0", 0, 12), vw("k3", 0, 12), 205.0, None, A_.mult)
            ts(vw("j1", 0, 12), vw("j0", 0, 12), 11, None, A_.logical_shift_right)
            ts(vw("k1", 0, 12), vw("j1", 0, 12), -10.0, None, A_.mult)
            ts(vw("k2", 0, 12), vw("j1", 0, 12), 32.0, E16, A_.mult, A_.add)
            tt(vw("k1", 0, 12), vw("k1", 0, 12), vw("k3", 0, 12), A_.add)
            ts(vw("k0", 0, 12), vw("k1", 0, 12), 8.0, -10.0, A_.is_ge, A_.mult)
            tt(vw("k1", 0, 12), vw("k1", 0, 12), vw("k2", 0, 12), A_.add)
            tt(vw("k1", 0, 12), vw("k1", 0, 12), vw("k0", 0, 12), A_.add)
            ts(vw("st", L_SF, L_SF + 12), vw("k1", 0, 12), 2.0, None, A_.add)
            cp("V", vw("ul", L_SI, L_END), vw("st", L_SI, L_END))
            quant("vq", "vs", 0, "vt", 0, 128)
        else:
            again(rd)
            for b in range(4):
                pull("VA"[b // 2], b, 384, 192)
            layer(384, 192)
            for b in range(4):
                relu(b, 384, 192)
                add(b, 384, 192, 128)
            quant(qn, sn, 384, "xn", 384, 192)
        if rd == 1:
            for b in range(4):
                mm(b, "eq", "es", 128 * b, qx, sx, 0, 384)
        if rd == 2:
            mm(4, "vq", "vs", 0, qn, sn, 384, 192)
            cp("A", vw("yo", 128, C), bank(4, 0, 192))
            for o, a in stores(128, 192):
                dma("S", o, a, "outs", NOUT)
            cp("V", vw("o0", 0, 32), vw(rl, 32, 64))
            ts(vw("o1", 0, 32), vw("o0", 0, 32), 13.0, None, A_.mult)
            ts(vw("o3", 0, 32), vw("o0", 0, 32), 240, None, A_.bitwise_and)
            ts(vw("o4", 0, 32), vw("o1", 0, 32), 15, None, A_.bitwise_and)
            tt(vw("opf", 0, 32), vw("o3", 0, 32), vw("o4", 0, 32), A_.add)
            for d in range(8):
                dma("S", hbm(T["op"][d:d + 1, 0:C - TURN]), vw("opf", 0, 32, 1, 16 * d + 2, 16 * d + 10), "outs", NOUT)
                dma("S", hbm(T["op"][d:d + 1, C - TURN:C]), vw("opf", 0, 32, 1, 16 * d, 16 * d + 2), "outs", NOUT)

        if rd < 2:
            cp("A", vw("si", 0, 256), ind(vw(rl, 0, 256), lst(L_SI + 16 * rd, 16)))
        cp("V", vw("i2", 192, 256), ind(vw(rl, 0, 96), lst(L_NB + 6 * rd, 4)))
        turn(vw("o2", 192, 256), vw("i2", 192, 256))
        again(rd)
        if rd == 2:
            for b in range(4):
                pull("VA"[b // 2], b, S, 128)
            layer(S, 128)
            for b in range(4):
                relu(b, S, 128)
                add(b, S, 128, 0)
            quant(qn, sn, S, "xn", S, 128)
            mm(4, "vq", "vs", 0, qn, sn, S, 128)
            one, two = stores(0, TURN), stores(TURN, TURN)
            for i in range(1, 6):
                dma("S", one[i][0], one[i][1], "outs", NOUT)
                dma("A", two[i][0], two[i][1], "outs", NOUT)
            cp("V", vw("yo", 0, 128), bank(4, 0, 128))
            dma("S", one[0][0], one[0][1], "outs", NOUT)
            dma("A", two[0][0], two[0][1], "outs", NOUT)
            break
        turn(vw("sw", 0, 256), vw("si", 0, 256))
        tt(vw("sg", 0, 80), ind(vw("sw", 0, 256), lst(L_SF + 6 * rd, 5)), vw("mk", 0, 80), A_.mult)
        scan(vw("sc", 0, 80), vw("rz", 0, 80), vw("sg", 0, 80))
        cp("V", vw("offp", 0, 16), vw("sc", 4, 80, 5))
        n, f0 = (C, 0) if rd == 0 else (128, S)
        for b in range(4):
            pull("AAVV"[b] if rd == 0 else "A", b, S, n)
        if rd == 1:
            pull("V", 0, 0, S)
        layer(S, n)
        pull("A", 1, 0, S)
        if rd == 0:
            pull("V", 0, 0, S)
        pull("V", 2, 0, S)
        relu(0, S, n)
        relu(1, S, n)
        pull("A", 3, 0, S)
        add(0, S, n, f0)
        add(1, S, n, f0)
        relu(2, S, n)
        relu(3, S, n)
        next_gather(k)
        quant("qy", "sy", 0, "yt", 0, S)
        add(2, S, n, f0)
        add(3, S, n, f0)
        for b in range(4):
            mm(4 + b, "wq", "wp", 128 * b, "qy", "sy", 0, S)
        if rd == 0:
            for b in range(4):
                mm(b, "eq", "es", 128 * b, qx, sx, 0, S)
        next_lists(k)
        for b in range(4):
            relu(b, 0, S)
            add(b, 0, S, 0)
        quant(qn, sn, 0, "xn", 0, S)
        quant(qn, sn, S, "xn", S, n)

    for q in count:
        wait("G", "e" + q, count[q])
    for sem in total:
        wait("G", sem, total[sem])
